import numpy as np
import ml_dtypes


def mxq(x, axis, fmt="e4m3"):
    dtype, down = {"e4m3": (ml_dtypes.float8_e4m3fn, 7), "e5m2": (ml_dtypes.float8_e5m2, 14)}[fmt]
    v = np.moveaxis(np.asarray(x, np.float32).astype(ml_dtypes.bfloat16).astype(np.float64), axis, -1)
    blocks = v.reshape(v.shape[:-1] + (-1, 32))
    amax = np.abs(blocks).max(-1, keepdims=True)
    byte = np.maximum(np.where(amax > 0, np.frexp(amax)[1] - 1 + 127, 0) - down, 1)
    scale = np.exp2(byte - 127.0)
    codes = (blocks / scale).astype(np.float32).astype(dtype).astype(np.float64)
    return np.moveaxis((codes * scale).reshape(v.shape), -1, axis)


WIDE = False


def mx_kscale(k):
    if not WIDE:
        return np.ones(k)
    levels = np.array([10, -10, 5, -5, 0])
    if k % 512:
        return np.exp2(np.random.permutation(np.resize(levels, k // 32))).repeat(32)
    a = np.empty((k // 512, 16))
    for p in range(k // 512):
        a[p, :8] = np.random.permutation(np.resize(levels, 8))
        for g in range(8):
            far = levels[np.abs(levels - a[p, g]) >= 10]
            a[p, g + 8] = far[np.random.randint(len(far))]
    return np.exp2(a.ravel()).repeat(32)


BF16 = ml_dtypes.bfloat16


def bf(x):
    return np.asarray(x, np.float32).astype(BF16)


def f64(x):
    return np.asarray(x).astype(np.float64)


E2M1 = np.array([0.0, 0.5, 1.0, 1.5, 2.0, 3.0, 4.0, 6.0, -0.0, -0.5, -1.0, -1.5, -2.0, -3.0, -4.0, -6.0])


def pack_weight(w, fmt):
    k, n = w.shape
    w = f64(bf(w)).reshape(k // 32, 32, n)
    amax = np.abs(w).max(1)
    if fmt == "e4m3":
        byte = np.frexp(amax)[1] - 1 + 127 - 7
    else:
        mant, ex = np.frexp(amax / 6.0)
        byte = np.where(mant > 0.5, ex, ex - 1) + 127
    byte = np.clip(np.where(amax > 0, byte, 1), 1, 254)
    scaled = (w * np.exp2(127.0 - byte)[:, None, :]).reshape(k, n).astype(np.float32)
    by_word = np.ascontiguousarray(scaled.reshape(k // 512, 128, 4, n).transpose(0, 1, 3, 2))
    if fmt == "e4m3":
        words = by_word.astype(ml_dtypes.float8_e4m3fn).view(np.uint8)
    else:
        c = by_word.astype(ml_dtypes.float4_e2m1fn).view(np.uint8) & 0xF
        words = c[..., 0::2] | (c[..., 1::2] << 4)
    return np.ascontiguousarray(words), np.ascontiguousarray(byte.astype(np.uint8).reshape(k // 512, 16, n))


def unpack_weight(words, scales, fmt):
    g, p, n, _ = words.shape
    if fmt == "e4m3":
        vals = np.ascontiguousarray(words).view(ml_dtypes.float8_e4m3fn).astype(np.float64)
    else:
        nib = np.empty((g, p, n, 4), np.uint8)
        nib[..., 0::2] = words & 0xF
        nib[..., 1::2] = words >> 4
        vals = E2M1[nib]
    vals = vals * np.repeat(np.exp2(scales.astype(np.float64) - 127.0), 8, axis=1)[..., None]
    return vals.transpose(0, 1, 3, 2).reshape(g * 512, n)
def pack4(w):
    words, scales = pack_weight(w, "e2m1")
    return words.reshape(words.shape[0], 128, -1), scales


def unpack4(words, scales):
    return unpack_weight(words.reshape(words.shape[0], 128, -1, 2), scales, "e2m1")


E4M3FN = np.array([(-1.0 if i & 128 else 1.0) * ((1.0 + (i & 7) / 8.0) * 2.0 ** (((i >> 3) & 15) - 7) if i & 120 else (i & 7) * 2.0 ** -9) for i in range(256)])


def e4m3fn_bytes(y):
    return np.clip(np.asarray(y, np.float64), -448.0, 448.0).astype(np.float32).astype(ml_dtypes.float8_e4m3fn).view(np.uint8)


def e4m3fn_values(b):
    return E4M3FN[b]


P, C, F, N, B = 1536, 1024, 2048, 512, 128


def setup_inputs():
    s, t = mx_kscale(C), mx_kscale(F)
    x = np.random.standard_normal((P, C)) * s
    x_scale = (np.abs(x).reshape(P, C // B, B).max(2) / 448).astype(np.float32)
    x_bytes = e4m3fn_bytes(x / np.repeat(f64(x_scale), B, 1))
    w1_words, w1_scales = pack4(np.random.standard_normal((C, F)) / np.sqrt(C) / s[:, None])
    w2 = np.random.standard_normal((N, F)) / np.sqrt(F) / t
    w2_scale = (np.abs(w2).reshape(N // B, B, F // B, B).max((1, 3)) / 448).astype(np.float32)
    w2_bytes = e4m3fn_bytes(w2 / np.repeat(np.repeat(f64(w2_scale), B, 0), B, 1))
    return {"x_bytes": x_bytes, "x_scale": x_scale,
            "w1_words": w1_words, "w1_scales": w1_scales,
            "scale": bf((1 + 0.1 * np.random.standard_normal(F)) * t),
            "shift": bf(0.3 * np.random.standard_normal(F) * t),
            "cap": bf((1.5 + 0.1 * np.random.standard_normal(F)) * t),
            "w2_bytes": w2_bytes, "w2_scale": w2_scale}


def reference(x_bytes, x_scale, w1_words, w1_scales, scale, shift, cap, w2_bytes, w2_scale):
    x = e4m3fn_values(x_bytes) * np.repeat(f64(x_scale), B, 1)
    w2 = e4m3fn_values(w2_bytes) * np.repeat(np.repeat(f64(w2_scale), B, 0), B, 1)
    z = mxq(x, 1, "e4m3") @ unpack4(w1_words, w1_scales)
    z = z * f64(scale) + f64(shift)
    h = np.minimum(np.maximum(z, 0), f64(cap))
    y = mxq(w2, 1, "e4m3") @ mxq(h, 1, "e4m3").T
    return y

@@ -1,0 +1,549 @@
+from contextlib import ExitStack
+
+import concourse.mybir as mybir
+from concourse.masks import make_identity
+
+F32 = mybir.dt.float32
+BF16 = mybir.dt.bfloat16
+I32 = mybir.dt.int32
+U32 = mybir.dt.uint32
+U8 = mybir.dt.uint8
+F8 = mybir.dt.float8_e4m3fn
+F8X4 = mybir.dt.float8_e4m3fn_x4
+F4X4 = mybir.dt.float4_e2m1fn_x4
+ALU = mybir.AluOpType
+ACT = mybir.ActivationFunctionType
+
+PIXELS, C_IN, HIDDEN, C_OUT = 1536, 1024, 2048, 512
+P = 128
+SLOTS = 4
+K_PASS = P * SLOTS
+PASSES = C_IN // K_PASS
+BUNDLES = HIDDEN // K_PASS
+GROUP = 512
+GROUPS = PIXELS // GROUP
+TILES = GROUP // P
+ROW_TILES = C_OUT // P
+BLOCK = 128
+UNITS = GROUPS * BUNDLES
+
+FLOPS = 2 * PIXELS * HIDDEN * (C_IN + C_OUT)
+
+JOBS = (
+    {
+        "tensor": (("x_turn", 1, 0), ("w2_turn", 0, 0), ("w2_turn", 1, 0)),
+        "scalar": ((("x_widen", 1, 0),), (), (("x_widen", 1, 3),)),
+        "vector": (
+            (("x_widen", 1, 1), ("x_widen", 1, 2), ("vectors", 0)),
+            (("w1", 1),),
+            (("w2_widen", 0, 0), ("w2_widen", 1, 0)),
+            (),
+        ),
+    },
+    {
+        "tensor": (("x_turn", 1, 1), ("x_turn", 1, 2), ("w2_turn", 0, 1)),
+        "scalar": ((("x_out", 1, 0), ("w2_out", 0, 0)), (), ()),
+        "vector": (
+            (("w1", 2), ("w2_widen", 0, 1), ("x_widen", 2, 0)),
+            (("w2_out", 1, 0), ("w1", 3)),
+            (("w2_widen", 1, 1),),
+            (),
+        ),
+    },
+    {
+        "tensor": (("x_turn", 1, 3), ("w2_turn", 1, 1)),
+        "scalar": ((("x_out", 1, 1), ("w2_out", 0, 1)), (("x_out", 1, 2),), ()),
+        "vector": ((), (("w2_widen", 2, 0), ("w2_widen", 2, 1)), (("x_widen", 2, 1),), (("x_widen", 2, 2),)),
+    },
+    {
+        "tensor": (("x_turn", 2, 0), ("w2_turn", 2, 0), ("w2_turn", 2, 1), ("x_turn", 2, 1)),
+        "scalar": ((("x_out", 1, 3), ("w2_out", 1, 1)), (), (("x_widen", 2, 3),)),
+        "vector": ((("x_quant", 1, 0), ("x_quant", 1, 1)), (), (), ()),
+    },
+    {
+        "tensor": (),
+        "scalar": ((("x_out", 2, 0), ("w2_out", 2, 0)), (), (("x_out", 2, 1),)),
+        "vector": ((), (("w2_widen", 3, 0),), (("w2_widen", 3, 1),), ()),
+    },
+    {
+        "tensor": (("w2_turn", 3, 0), ("x_turn", 2, 2), ("x_turn", 2, 3), ("w2_turn", 3, 1)),
+        "scalar": ((("w2_out", 2, 1),), (), ()),
+        "vector": ((("w2_quant", 0),), (), (), ()),
+    },
+    {
+        "tensor": (),
+        "scalar": ((("w2_out", 3, 0), ("w2_out", 3, 1)), (), (("x_out", 2, 2),)),
+        "vector": ((("w2_quant", 1),), (("w2_quant", 2), ("w2_quant", 3)), (), ()),
+    },
+    {
+        "tensor": (("y_sum", 0, 0), ("y_sum", 0, 1), ("y_sum", 0, 2), ("y_sum", 0, 3)),
+        "scalar": ((("x_out", 2, 3),), (), ()),
+        "vector": ((("x_quant", 2, 0),), (("x_quant", 2, 1),), (), ()),
+    },
+    {
+        "tensor": (),
+        "scalar": ((), (), (("y_out", 0, 0), ("y_out", 0, 1))),
+        "vector": ((("y_out", 0, 3),), (), (), ()),
+    },
+    {
+        "tensor": (("y_sum", 1, 0), ("y_sum", 1, 1)),
+        "scalar": ((), (("y_out", 0, 2),), ()),
+        "vector": ((), (), (), ()),
+    },
+    {
+        "tensor": (("y_sum", 1, 2), ("y_sum", 1, 3)),
+        "scalar": ((("y_out", 1, 1),), (), ()),
+        "vector": ((), (), (), ()),
+    },
+    {
+        "tensor": (),
+        "scalar": ((("y_out", 1, 3),), (), ()),
+        "vector": ((("y_out", 1, 0),), (), (), (("y_out", 1, 2),)),
+    },
+)
+AT_ONCE = (0, 1, 3)
+
+
+def tile_clipped_pointwise_pair_d6_kernel(
+    tc, x_bytes, x_scale, w1_words, w1_scales, scale, shift, cap, w2_bytes, w2_scale, out
+):
+    nc = tc.nc
+    with ExitStack() as ctx:
+        keep = ctx.enter_context(tc.tile_pool(name="keep", bufs=1))
+        work = ctx.enter_context(tc.tile_pool(name="work", bufs=3))
+        psum = ctx.enter_context(tc.psum_pool(name="psum", bufs=1))
+        ctx.enter_context(tc.manual_schedule())
+
+        turn_order = ("x0", "x1", "y0", "y1")
+        turns = []
+
+        def next_bank():
+            turns.append(turn_order[len(turns) % 4])
+            return turns[-1]
+
+        def kept(shape, dtype, name):
+            return keep.tile(shape, dtype, name=name, align_bytes=64)
+
+        xb = [kept([P, TILES, C_IN], U8, "xb%d" % a) for a in range(GROUPS)]
+        xs = kept([P, GROUPS, TILES * C_IN // BLOCK], F32, "xs")
+        w1_raw = [kept([P, PASSES, 2 * K_PASS], U8, "w1_raw%d" % f) for f in range(BUNDLES)]
+        w1s_raw = kept([P, PASSES, HIDDEN], U8, "w1s_raw")
+        w2b = [kept([P, 2, HIDDEN], U8, "w2b%d" % h) for h in range(2)]
+        w2s = kept([P, ROW_TILES * HIDDEN // BLOCK], F32, "w2s")
+        vec_rows = kept([P, K_PASS], BF16, "vec_rows")
+        warm = kept([P, 512], BF16, "warm")
+        ident = kept([P, P], F32, "ident")
+
+        nc.vector.memset(warm[:], 0.0)
+        nc.vector.memset(vec_rows[:], 0.0)
+        nc.vector.memset(w1s_raw[:].rearrange("p g n -> p (g n)").bitcast(I32), 0)
+        make_identity(nc, ident[:])
+
+        x_src = x_bytes.rearrange("(a h p n) k -> a h p n k", h=2, p=P, n=2)
+        w1_src = w1_words.bitcast(I32)
+        w1s_src = w1_scales.bitcast(I32)
+        w1s_words = w1s_raw[:].bitcast(I32)
+        w2_src = w2_bytes.rearrange("(h i p) k -> h p i k", h=2, p=P)
+
+        def load_x(a):
+            nc.sync.dma_start(
+                out=xb[a][:].rearrange("p (h n) k -> p h (n k)", h=2), in_=x_src[a].rearrange("h p n k -> p h (n k)")
+            )
+
+        def load_w1(f):
+            nc.sync.dma_start(
+                out=w1_raw[f][:].bitcast(I32), in_=w1_src[:, :, 256 * f : 256 * f + 256].rearrange("g p c -> p g c")
+            )
+
+        nc.sync.dma_start(out=xb[0][:, 0:2, :], in_=x_src[0, 0])
+        nc.scalar.dma_start(
+            out=xs[:].rearrange("p a (h c) -> p (a h) c", h=2),
+            in_=x_scale.rearrange("(a h p n) j -> p (a h) (n j)", h=2, p=P, n=2),
+        )
+        nc.sync.dma_start(out=xb[0][:, 2:4, :], in_=x_src[0, 1])
+        load_w1(0)
+        for q in range(4):
+            nc.sync.dma_start(
+                out=w1s_words[32 * q : 32 * q + 4, :, :],
+                in_=w1s_src[:, 4 * q : 4 * q + 4, :].rearrange("g r c -> r g c"),
+            )
+        load_x(1)
+        for v, vec in enumerate((scale, shift, cap)):
+            nc.sync.dma_start(
+                out=vec_rows[BUNDLES * v : BUNDLES * v + BUNDLES, :], in_=vec.rearrange("(f c) -> f c", f=BUNDLES)
+            )
+        nc.sync.dma_start(out=w2s[:], in_=w2_scale.rearrange("i j -> (i j)").partition_broadcast(P))
+        load_w1(1)
+        nc.sync.dma_start(out=w2b[0][:], in_=w2_src[0])
+        nc.sync.dma_start(out=w2b[1][:], in_=w2_src[1])
+        load_w1(2)
+        load_w1(3)
+        load_x(2)
+
+        w1c = [kept([P, PASSES, 2 * K_PASS], U8, "w1c%d" % f) for f in range(BUNDLES)]
+        w1s = [kept([P, PASSES, K_PASS], U8, "w1s%d" % f) for f in range(BUNDLES)]
+        w2q = [kept([P, C_OUT], U32, "w2q%d" % f) for f in range(BUNDLES)]
+        w2qs = [kept([P, C_OUT], U8, "w2qs%d" % f) for f in range(BUNDLES)]
+        xq = [kept([P, PASSES, GROUP], U32, "xq%d" % a) for a in range(GROUPS)]
+        xqs = [kept([P, PASSES, GROUP], U8, "xqs%d" % a) for a in range(GROUPS)]
+
+        def w1_words_permute(f):
+            nc.vector.tensor_copy(
+                out=w1c[f][:].bitcast(I32).rearrange("p g (t c j) -> p g t c j", t=SLOTS, c=32),
+                in_=w1_raw[f][:].bitcast(I32).rearrange("p g (c t j) -> p g t c j", t=SLOTS, c=32),
+            )
+
+        def w1_scales_permute(f):
+            nc.vector.tensor_copy(
+                out=w1s[f][:].bitcast(I32).rearrange("p g (t c) -> p g t c", t=SLOTS),
+                in_=w1s_words[:, :, 128 * f : 128 * f + 128].rearrange("p g (c t) -> p g t c", t=SLOTS),
+            )
+
+        def w1_permute(engine, f):
+            w1_scales_permute(f)
+            w1_words_permute(f)
+
+        vec_turned = kept([P, SLOTS, P], F32, "vec_turned")
+        vecs = kept([P, SLOTS, 3 * BUNDLES], F32, "vecs")
+        vec_bank = []
+
+        def vectors_permute():
+            nc.vector.tensor_copy(
+                out=vec_turned[:].rearrange("p t (c i) -> p t c i", c=32),
+                in_=vec_rows[:].rearrange("p (c t i) -> p t c i", t=SLOTS, c=32),
+            )
+
+        def vectors_turn():
+            bank = psum.tile([P, SLOTS, P], F32, name="vec_bank", tag="x0")
+            vec_bank.append(bank)
+            for t in range(SLOTS):
+                nc.tensor.transpose(bank[:, t, :], vec_turned[:, t, :], ident[:])
+
+        def vectors_out(engine, part):
+            nc.vector.tensor_copy(out=vecs[:], in_=vec_bank[part][:, :, 0 : 3 * BUNDLES])
+
+        def scale_of(f, t):
+            return vecs[:, t, f : f + 1]
+
+        def shift_of(f, t):
+            return vecs[:, t, BUNDLES + f : BUNDLES + f + 1]
+
+        def cap_of(f, t):
+            return vecs[:, t, 2 * BUNDLES + f : 2 * BUNDLES + f + 1]
+
+        x_wide = {}
+        x_split = set()
+        x_bank = {}
+        x_grouped = {}
+
+        def copy(engine, out_, in_):
+            if engine == "vector":
+                nc.vector.tensor_copy(out=out_, in_=in_)
+            else:
+                nc.scalar.copy(out=out_, in_=in_)
+
+        def x_widen(engine, a, n, blocks=range(C_IN // BLOCK)):
+            if (a, n) not in x_wide:
+                x_wide[a, n] = work.tile([P, C_IN], BF16, name="x_wide", bufs=5, align_bytes=64)
+            wide = x_wide[a, n]
+            for j in blocks:
+                src = xb[a][:, n, BLOCK * j : BLOCK * j + BLOCK].bitcast(F8)
+                factor = xs[:, a, 8 * n + j : 8 * n + j + 1]
+                if engine == "vector":
+                    g, q = j // 4, j % 4
+                    x_split.add((a, n, g))
+                    halves = wide[:, K_PASS * g : K_PASS * (g + 1)].rearrange("p (u c e) -> p c u e", u=2, e=2)
+                    nc.vector.tensor_scalar(
+                        out=halves[:, 32 * q : 32 * q + 32, :, :],
+                        in0=src.rearrange("p (c u e) -> p c u e", u=2, e=2),
+                        scalar1=factor,
+                        scalar2=None,
+                        op0=ALU.mult,
+                    )
+                else:
+                    nc.scalar.activation(
+                        out=wide[:, BLOCK * j : BLOCK * j + BLOCK], in_=src, func=ACT.Copy, scale=factor
+                    )
+
+        def x_turn(a, n, tag):
+            words = x_wide[a, n][:].bitcast(F32)
+            bank = psum.tile([P, 4, P], F32, name="x_bank_" + tag, tag=tag)
+            x_bank[a, n] = bank
+            for g in range(PASSES):
+                for u in range(2):
+                    if (a, n, g) in x_split:
+                        src = words[:, 256 * g + 128 * u : 256 * g + 128 * u + 128]
+                    else:
+                        src = words[:, 256 * g + u : 256 * (g + 1) : 2]
+                    nc.tensor.transpose(bank[:, 2 * g + u, :], src, ident[:])
+
+        def x_out(engine, a, n):
+            if a not in x_grouped:
+                x_grouped[a] = work.tile([P, PASSES, SLOTS * GROUP], BF16, name="x_grouped", bufs=2, align_bytes=64)
+            words = x_grouped[a][:].bitcast(F32)[:, :, 256 * n : 256 * n + 256]
+            copy(
+                engine,
+                words.rearrange("p g (r u) -> p g r u", u=2),
+                x_bank[a, n][:].rearrange("p (g u) r -> p g r u", g=PASSES),
+            )
+
+        def x_quant(engine, a, g):
+            nc.vector.quantize_mx(out=xq[a][:, g, :].bitcast(F8X4), scales=xqs[a][:, g, :], in_=x_grouped[a][:, g, :])
+
+        def x_quant_tile(a, n):
+            c = slice(P * n, P * n + P)
+            for g in range(PASSES):
+                nc.vector.quantize_mx(
+                    out=xq[a][:, g, c].bitcast(F8X4),
+                    scales=xqs[a][:, g, c],
+                    in_=x_grouped[a][:, g, SLOTS * P * n : SLOTS * P * (n + 1)],
+                )
+
+        w2_wide = {}
+        w2_bank = {}
+        w2_grouped = {}
+
+        def w2_widen(engine, f, h):
+            for r in range(2):
+                wide = work.tile([P, K_PASS], BF16, name="w2_wide", bufs=8, align_bytes=64)
+                w2_wide[f, h, r] = wide
+                for q in range(4):
+                    k0 = K_PASS * f + BLOCK * q
+                    j = (2 * h + r) * (HIDDEN // BLOCK) + 4 * f + q
+                    nc.vector.tensor_scalar(
+                        out=wide[:, BLOCK * q : BLOCK * q + BLOCK].rearrange("p (c i t) -> p c t i", c=8, i=4),
+                        in0=w2b[h][:, r, k0 : k0 + BLOCK].bitcast(F8).rearrange("p (c t i) -> p c t i", c=8, i=4),
+                        scalar1=w2s[:, j : j + 1],
+                        scalar2=None,
+                        op0=ALU.mult,
+                    )
+
+        def w2_turn(f, h, tag):
+            bank = psum.tile([P, 4, P], F32, name="w2_bank_" + tag, tag=tag)
+            w2_bank[f, h] = bank
+            for r in range(2):
+                words = w2_wide[f, h, r][:].bitcast(F32)
+                for u in range(2):
+                    nc.tensor.transpose(bank[:, 2 * r + u, :], words[:, u::2], ident[:])
+
+        def w2_out(engine, f, h):
+            if f not in w2_grouped:
+                w2_grouped[f] = work.tile([P, SLOTS * C_OUT], BF16, name="w2_grouped", bufs=4, align_bytes=64)
+            words = w2_grouped[f][:].bitcast(F32)[:, 512 * h : 512 * h + 512]
+            copy(
+                engine,
+                words.rearrange("p (r c u) -> p r c u", r=2, u=2),
+                w2_bank[f, h][:].rearrange("p (r u) c -> p r c u", r=2),
+            )
+
+        def w2_quant(engine, f):
+            nc.vector.quantize_mx(out=w2q[f][:].bitcast(F8X4), scales=w2qs[f][:], in_=w2_grouped[f][:])
+
+        z = {}
+        planes = {}
+        grouped = {}
+        hq = {}
+        hqs = {}
+
+        def z_sum(a, f, columns):
+            for t in range(SLOTS):
+                for g in range(PASSES):
+                    nc.tensor.matmul_mx(
+                        out=z[t][:, columns],
+                        lhsT=w1c[f][:, g, 2 * P * t : 2 * P * (t + 1)].bitcast(F4X4),
+                        lhsT_scale=w1s[f][:, g, P * t : P * (t + 1)],
+                        rhs=xq[a][:, g, columns].bitcast(F8X4),
+                        rhs_scale=xqs[a][:, g, columns],
+                        start=(g == 0),
+                        stop=(g == PASSES - 1),
+                    )
+
+        def z_banks():
+            for t in range(SLOTS):
+                z[t] = psum.tile([P, GROUP], F32, name="z%d" % t, tag="z%d" % t)
+
+        def relu(m, t):
+            f = m % BUNDLES
+            if m not in planes:
+                planes[m] = work.tile([P, SLOTS, GROUP], BF16, name="planes", align_bytes=64)
+            nc.scalar.activation(
+                out=planes[m][:, t, :], in_=z[t][:], func=ACT.Relu, bias=shift_of(f, t), scale=scale_of(f, t)
+            )
+
+        def clip(m, t, c0=0, c1=GROUP):
+            part = planes[m][:, t, c0:c1]
+            nc.vector.tensor_scalar(
+                out=part, in0=part, scalar1=0.0, scalar2=cap_of(m % BUNDLES, t), op0=ALU.max, op1=ALU.min
+            )
+
+        def interleave(m, c0=0, c1=GROUP):
+            if m not in grouped:
+                grouped[m] = work.tile([P, SLOTS * GROUP], BF16, name="grouped", align_bytes=64)
+            nc.vector.tensor_copy(
+                out=grouped[m][:, SLOTS * c0 : SLOTS * c1].rearrange("p (c i t) -> p c t i", i=4, t=SLOTS),
+                in_=planes[m][:, :, c0:c1].rearrange("p t (c i) -> p c t i", i=4),
+            )
+
+        def h_quant(m, c0=0, c1=GROUP):
+            if m not in hq:
+                hq[m] = work.tile([P, GROUP], U32, name="hq", bufs=8, align_bytes=64)
+                hqs[m] = work.tile([P, GROUP], U8, name="hqs", bufs=8, align_bytes=64)
+            nc.vector.quantize_mx(
+                out=hq[m][:, c0:c1].bitcast(F8X4), scales=hqs[m][:, c0:c1], in_=grouped[m][:, SLOTS * c0 : SLOTS * c1]
+            )
+
+        y = {}
+
+        def y_pass(bank, a, i, f, c0=0, c1=GROUP):
+            m = BUNDLES * a + f
+            nc.tensor.matmul_mx(
+                out=bank[:],
+                lhsT=w2q[f][:, P * i : P * (i + 1)].bitcast(F8X4),
+                lhsT_scale=w2qs[f][:, P * i : P * (i + 1)],
+                rhs=hq[m][:, c0:c1].bitcast(F8X4),
+                rhs_scale=hqs[m][:, c0:c1],
+                start=(f == 0),
+                stop=(f == BUNDLES - 1),
+            )
+
+        def y_sum(a, i, tag):
+            y[a, i] = psum.tile([P, GROUP], F32, name="y_" + tag, tag=tag)
+            for f in range(BUNDLES):
+                y_pass(y[a, i], a, i, f)
+
+        def y_out(engine, a, i):
+            rows = work.tile([P, GROUP], F32, name="y_rows", bufs=4, align_bytes=64)
+            copy(
+                engine,
+                rows[:].rearrange("m (h r n) -> m h r n", h=2, n=2),
+                y[a, i][:].rearrange("m (h n r) -> m h r n", h=2, n=2),
+            )
+            nc.sync.dma_start(out=out[P * i : P * (i + 1), GROUP * a : GROUP * (a + 1)], in_=rows[:])
+
+        def y_half_out(engine, bank, a, i, h):
+            rows = work.tile([P, 256], F32, name="y_half", bufs=8, align_bytes=64)
+            copy(engine, rows[:].rearrange("m (r n) -> m r n", n=2), bank[:].rearrange("m (n r) -> m r n", n=2))
+            c0 = GROUP * a + 256 * h
+            nc.sync.dma_start(out=out[P * i : P * (i + 1), c0 : c0 + 256], in_=rows[:])
+
+        warm_bank = psum.tile([P, 512], F32, name="warm_bank", tag="z3")
+
+        def warm_up(count):
+            for k in range(count):
+                nc.tensor.matmul(out=warm_bank[:], lhsT=warm[:, 0:P], rhs=warm[:], start=True, stop=True)
+
+        warm_up(5)
+        x_widen("vector", 0, 0)
+        x_widen("scalar", 0, 1)
+        x_turn(0, 0, "x0")
+        warm_up(1)
+        x_widen("vector", 0, 2)
+        x_out("vector", 0, 0)
+        x_turn(0, 1, "x1")
+        x_widen("vector", 0, 3, range(0, 4))
+        x_widen("scalar", 0, 3, range(4, 8))
+        warm_up(1)
+        x_turn(0, 2, "y0")
+        warm_up(1)
+        x_quant_tile(0, 0)
+        x_out("scalar", 0, 1)
+        w1_words_permute(0)
+        w1_scales_permute(0)
+        x_out("vector", 0, 2)
+        x_turn(0, 3, "y1")
+        warm_up(1)
+        z_banks()
+        z_sum(0, 0, slice(0, P))
+        x_quant_tile(0, 1)
+        z_sum(0, 0, slice(P, 2 * P))
+        x_out("scalar", 0, 3)
+        x_quant_tile(0, 2)
+        x_quant_tile(0, 3)
+        vectors_permute()
+        vectors_turn()
+        z_sum(0, 0, slice(2 * P, 3 * P))
+        z_sum(0, 0, slice(3 * P, 4 * P))
+
+        engine_jobs = {
+            "x_widen": x_widen,
+            "x_out": x_out,
+            "x_quant": x_quant,
+            "w1": w1_permute,
+            "w2_widen": w2_widen,
+            "w2_out": w2_out,
+            "w2_quant": w2_quant,
+            "vectors": vectors_out,
+            "y_out": y_out,
+        }
+        tensor_jobs = {"x_turn": x_turn, "w2_turn": w2_turn, "y_sum": y_sum}
+
+        def run(engine, jobs):
+            for job in jobs:
+                engine_jobs[job[0]](engine, *job[1:])
+
+        unclipped = []
+        unquantized = []
+
+        def quantize_waiting():
+            for k in unquantized:
+                h_quant(k)
+            unquantized.clear()
+
+        for m in range(UNITS):
+            scalar, vector = JOBS[m]["scalar"], JOBS[m]["vector"]
+            run("scalar", scalar[0])
+            if m > 0:
+                z_banks()
+                z_sum(m // BUNDLES, m % BUNDLES, slice(0, GROUP))
+            run("vector", vector[0])
+            for k in unclipped:
+                for t in range(SLOTS):
+                    clip(k, t)
+                quantize_waiting()
+            run("vector", vector[1])
+            for k in unclipped:
+                interleave(k)
+                unquantized.append(k)
+            unclipped.clear()
+            run("vector", vector[2])
+            for t in range(SLOTS):
+                if t == 2:
+                    run("scalar", scalar[1])
+                relu(m, t)
+                if m in AT_ONCE:
+                    clip(m, t)
+            if m in AT_ONCE:
+                quantize_waiting()
+                interleave(m)
+                unquantized.append(m)
+            else:
+                unclipped.append(m)
+            if m == UNITS - 1:
+                quantize_waiting()
+            run("scalar", scalar[2])
+            run("vector", vector[3])
+            for job in JOBS[m]["tensor"]:
+                tensor_jobs[job[0]](*job[1:], next_bank())
+
+        last, a = UNITS - 1, GROUPS - 1
+        halves = (slice(0, 256), slice(256, GROUP))
+        for t in range(SLOTS):
+            clip(last, t, 0, 256)
+        interleave(last, 0, 256)
+        for t in range(SLOTS):
+            clip(last, t, 256, GROUP)
+        h_quant(last, 0, 256)
+        interleave(last, 256, GROUP)
+        y_half = {}
+        for h in range(2):
+            for i in range(ROW_TILES):
+                tag = next_bank() if h == 0 else "z%d" % i
+                y_half[h, i] = psum.tile([P, 256], F32, name="y_half_" + tag, tag=tag)
+                for f in range(BUNDLES - 1):
+                    y_pass(y_half[h, i], a, i, f, halves[h].start, halves[h].stop)
+        for h in range(2):
+            if h == 1:
+                h_quant(last, 256, GROUP)
+            for i in range(ROW_TILES):
+                y_pass(y_half[h, i], a, i, BUNDLES - 1, halves[h].start, halves[h].stop)
+                y_half_out("vector" if h == 1 and i % 2 == 1 else "scalar", y_half[h, i], a, i, h)

@@ -31,77 +31,86 @@ FLOPS = 2 * PIXELS * HIDDEN * (C_IN + C_OUT)
 
 JOBS = (
     {
-        "tensor": (("x_turn", 1, 0), ("w2_turn", 0, 0), ("w2_turn", 1, 0)),
-        "scalar": ((("x_widen", 1, 0),), (), (("x_widen", 1, 3),)),
+        "tensor": (("x_turn", 1, 0), ("x_turn", 1, 1), ("x_turn", 1, 2), ("w2_turn", 0, 0)),
+        "scalar": ((("x_widen", 1, 2), ("x_widen", 1, 0)), (), ()),
+        "chains": (),
         "vector": (
-            (("x_widen", 1, 1), ("x_widen", 1, 2), ("vectors", 0)),
-            (("w1", 1),),
-            (("w2_widen", 0, 0), ("w2_widen", 1, 0)),
+            (("x_widen", 1, 1), ("x_widen", 1, 3), ("vectors",), ("w1", 1), ("w2_widen", 0, 0), ("w2_widen", 1, 0)),
+            (),
             (),
         ),
     },
     {
-        "tensor": (("x_turn", 1, 1), ("x_turn", 1, 2), ("w2_turn", 0, 1)),
-        "scalar": ((("x_out", 1, 0), ("w2_out", 0, 0)), (), ()),
+        "tensor": (("w2_turn", 1, 0), ("x_turn", 1, 3), ("w2_turn", 0, 1)),
+        "scalar": ((("x_out", 1, 1), ("x_out", 1, 0)), (("x_out", 1, 2),), (("w2_out", 0, 0),)),
+        "chains": (0,),
+        "vector": ((("w2_widen", 0, 1),), (("w2_widen", 3, 1), ("w1", 2)), (("w2_widen", 2, 0),)),
+    },
+    {
+        "tensor": (("w2_turn", 2, 0), ("w2_turn", 3, 1)),
+        "scalar": ((), (("w2_out", 1, 0), ("w2_out", 0, 1)), ()),
+        "chains": (),
+        "vector": ((("x_out", 1, 3), ("w1", 3)), (), ()),
+    },
+    {
+        "tensor": (),
+        "scalar": ((), (), (("w2_out", 3, 1),)),
+        "chains": (1, 2),
         "vector": (
-            (("w1", 2), ("w2_widen", 0, 1), ("x_widen", 2, 0)),
-            (("w2_out", 1, 0), ("w1", 3)),
-            (("w2_widen", 1, 1),),
+            (("w2_widen", 3, 0), ("x_quant", 1, 1), ("x_quant", 1, 0), ("w2_widen", 2, 1), ("w2_widen", 1, 1)),
             (),
+            (("x_widen", 2, 1),),
         ),
     },
     {
-        "tensor": (("x_turn", 1, 3), ("w2_turn", 1, 1)),
-        "scalar": ((("x_out", 1, 1), ("w2_out", 0, 1)), (("x_out", 1, 2),), ()),
-        "vector": ((), (("w2_widen", 2, 0), ("w2_widen", 2, 1)), (("x_widen", 2, 1),), (("x_widen", 2, 2),)),
+        "tensor": (("w2_turn", 2, 1), ("w2_turn", 1, 1), ("w2_turn", 3, 0)),
+        "scalar": ((("w2_out", 2, 0),), (("x_widen", 2, 2),), ()),
+        "chains": (),
+        "vector": ((("x_widen", 2, 0),), (), ()),
     },
     {
-        "tensor": (("x_turn", 2, 0), ("w2_turn", 2, 0), ("w2_turn", 2, 1), ("x_turn", 2, 1)),
-        "scalar": ((("x_out", 1, 3), ("w2_out", 1, 1)), (), (("x_widen", 2, 3),)),
-        "vector": ((("x_quant", 1, 0), ("x_quant", 1, 1)), (), (), ()),
+        "tensor": (("x_turn", 2, 0), ("x_turn", 2, 1), ("x_turn", 2, 2)),
+        "scalar": ((("w2_out", 2, 1), ("w2_out", 1, 1)), (), ()),
+        "chains": (),
+        "vector": ((("x_widen", 2, 3), ("w2_quant", 0), ("w2_out", 3, 0)), (), ()),
     },
     {
-        "tensor": (),
-        "scalar": ((("x_out", 2, 0), ("w2_out", 2, 0)), (), (("x_out", 2, 1),)),
-        "vector": ((), (("w2_widen", 3, 0),), (("w2_widen", 3, 1),), ()),
+        "tensor": (("x_turn", 2, 3),),
+        "scalar": ((), (("x_out", 2, 2),), (("x_out", 2, 0),)),
+        "chains": (3,),
+        "vector": ((), (("w2_quant", 3),), ()),
     },
     {
-        "tensor": (("w2_turn", 3, 0), ("x_turn", 2, 2), ("x_turn", 2, 3), ("w2_turn", 3, 1)),
-        "scalar": ((("w2_out", 2, 1),), (), ()),
-        "vector": ((("w2_quant", 0),), (), (), ()),
-    },
-    {
-        "tensor": (),
-        "scalar": ((("w2_out", 3, 0), ("w2_out", 3, 1)), (), (("x_out", 2, 2),)),
-        "vector": ((("w2_quant", 1),), (("w2_quant", 2), ("w2_quant", 3)), (), ()),
-    },
-    {
-        "tensor": (("y_sum", 0, 0), ("y_sum", 0, 1), ("y_sum", 0, 2), ("y_sum", 0, 3)),
-        "scalar": ((("x_out", 2, 3),), (), ()),
-        "vector": ((("x_quant", 2, 0),), (("x_quant", 2, 1),), (), ()),
+        "tensor": (("y_sum", 0, 0), ("y_sum", 0, 1), ("y_sum", 0, 2)),
+        "scalar": ((("x_out", 2, 3), ("x_out", 2, 1)), (), ()),
+        "chains": (4,),
+        "vector": ((("w2_quant", 2),), (("w2_quant", 1),), (("x_quant", 2, 1), ("x_quant", 2, 0))),
     },
     {
         "tensor": (),
-        "scalar": ((), (), (("y_out", 0, 0), ("y_out", 0, 1))),
-        "vector": ((("y_out", 0, 3),), (), (), ()),
+        "scalar": ((), (), ()),
+        "chains": (5,),
+        "vector": ((), (), ()),
     },
     {
-        "tensor": (("y_sum", 1, 0), ("y_sum", 1, 1)),
-        "scalar": ((), (("y_out", 0, 2),), ()),
-        "vector": ((), (), (), ()),
+        "tensor": (("y_sum", 0, 3),),
+        "scalar": ((("y_out", 0, 2),), (), (("y_out", 0, 0),)),
+        "chains": (6, 7),
+        "vector": ((), (), ()),
     },
     {
-        "tensor": (("y_sum", 1, 2), ("y_sum", 1, 3)),
-        "scalar": ((("y_out", 1, 1),), (), ()),
-        "vector": ((), (), (), ()),
+        "tensor": (("y_sum", 1, 0), ("y_sum", 1, 1), ("y_sum", 1, 2), ("y_sum", 1, 3)),
+        "scalar": ((), (("y_out", 0, 3), ("y_out", 0, 1)), ()),
+        "chains": (8,),
+        "vector": ((), (), ()),
     },
     {
         "tensor": (),
-        "scalar": ((("y_out", 1, 3),), (), ()),
-        "vector": ((("y_out", 1, 0),), (), (), (("y_out", 1, 2),)),
+        "scalar": ((("y_out", 1, 0), ("y_out", 1, 1), ("y_out", 1, 2), ("y_out", 1, 3)), (), ()),
+        "chains": (9, 10),
+        "vector": ((), (), ()),
     },
 )
-AT_ONCE = (0, 1, 3)
 
 
 def tile_clipped_pointwise_pair_d6_kernel(
@@ -131,10 +140,8 @@ def tile_clipped_pointwise_pair_d6_kernel(
         w2b = [kept([P, 2, HIDDEN], U8, "w2b%d" % h) for h in range(2)]
         w2s = kept([P, ROW_TILES * HIDDEN // BLOCK], F32, "w2s")
         vec_rows = kept([P, K_PASS], BF16, "vec_rows")
-        warm = kept([P, 512], BF16, "warm")
         ident = kept([P, P], F32, "ident")
 
-        nc.vector.memset(warm[:], 0.0)
         nc.vector.memset(vec_rows[:], 0.0)
         nc.vector.memset(w1s_raw[:].rearrange("p g n -> p (g n)").bitcast(I32), 0)
         make_identity(nc, ident[:])
@@ -219,8 +226,8 @@ def tile_clipped_pointwise_pair_d6_kernel(
             for t in range(SLOTS):
                 nc.tensor.transpose(bank[:, t, :], vec_turned[:, t, :], ident[:])
 
-        def vectors_out(engine, part):
-            nc.vector.tensor_copy(out=vecs[:], in_=vec_bank[part][:, :, 0 : 3 * BUNDLES])
+        def vectors_out(engine):
+            nc.vector.tensor_copy(out=vecs[:], in_=vec_bank[0][:, :, 0 : 3 * BUNDLES])
 
         def scale_of(f, t):
             return vecs[:, t, f : f + 1]
@@ -365,7 +372,7 @@ def tile_clipped_pointwise_pair_d6_kernel(
         def relu(m, t):
             f = m % BUNDLES
             if m not in planes:
-                planes[m] = work.tile([P, SLOTS, GROUP], BF16, name="planes", align_bytes=64)
+                planes[m] = work.tile([P, SLOTS, GROUP], BF16, name="planes", bufs=5, align_bytes=64)
             nc.scalar.activation(
                 out=planes[m][:, t, :], in_=z[t][:], func=ACT.Relu, bias=shift_of(f, t), scale=scale_of(f, t)
             )
@@ -386,8 +393,8 @@ def tile_clipped_pointwise_pair_d6_kernel(
 
         def h_quant(m, c0=0, c1=GROUP):
             if m not in hq:
-                hq[m] = work.tile([P, GROUP], U32, name="hq", bufs=8, align_bytes=64)
-                hqs[m] = work.tile([P, GROUP], U8, name="hqs", bufs=8, align_bytes=64)
+                hq[m] = work.tile([P, GROUP], U32, name="hq", bufs=9, align_bytes=64)
+                hqs[m] = work.tile([P, GROUP], U8, name="hqs", bufs=9, align_bytes=64)
             nc.vector.quantize_mx(
                 out=hq[m][:, c0:c1].bitcast(F8X4), scales=hqs[m][:, c0:c1], in_=grouped[m][:, SLOTS * c0 : SLOTS * c1]
             )
@@ -426,32 +433,21 @@ def tile_clipped_pointwise_pair_d6_kernel(
             c0 = GROUP * a + 256 * h
             nc.sync.dma_start(out=out[P * i : P * (i + 1), c0 : c0 + 256], in_=rows[:])
 
-        warm_bank = psum.tile([P, 512], F32, name="warm_bank", tag="z3")
-
-        def warm_up(count):
-            for k in range(count):
-                nc.tensor.matmul(out=warm_bank[:], lhsT=warm[:, 0:P], rhs=warm[:], start=True, stop=True)
-
-        warm_up(5)
         x_widen("vector", 0, 0)
         x_widen("scalar", 0, 1)
         x_turn(0, 0, "x0")
-        warm_up(1)
         x_widen("vector", 0, 2)
         x_out("vector", 0, 0)
         x_turn(0, 1, "x1")
         x_widen("vector", 0, 3, range(0, 4))
         x_widen("scalar", 0, 3, range(4, 8))
-        warm_up(1)
         x_turn(0, 2, "y0")
-        warm_up(1)
         x_quant_tile(0, 0)
         x_out("scalar", 0, 1)
         w1_words_permute(0)
         w1_scales_permute(0)
         x_out("vector", 0, 2)
         x_turn(0, 3, "y1")
-        warm_up(1)
         z_banks()
         z_sum(0, 0, slice(0, P))
         x_quant_tile(0, 1)
@@ -481,7 +477,6 @@ def tile_clipped_pointwise_pair_d6_kernel(
             for job in jobs:
                 engine_jobs[job[0]](engine, *job[1:])
 
-        unclipped = []
         unquantized = []
 
         def quantize_waiting():
@@ -490,40 +485,31 @@ def tile_clipped_pointwise_pair_d6_kernel(
             unquantized.clear()
 
         for m in range(UNITS):
-            scalar, vector = JOBS[m]["scalar"], JOBS[m]["vector"]
-            run("scalar", scalar[0])
+            jobs = JOBS[m]
+            scalar_before, scalar_between, scalar_after = jobs["scalar"]
+            vector_before, vector_between, vector_after = jobs["vector"]
+            run("scalar", scalar_before)
             if m > 0:
                 z_banks()
                 z_sum(m // BUNDLES, m % BUNDLES, slice(0, GROUP))
-            run("vector", vector[0])
-            for k in unclipped:
+            run("vector", vector_before)
+            for k in jobs["chains"]:
                 for t in range(SLOTS):
                     clip(k, t)
                 quantize_waiting()
-            run("vector", vector[1])
-            for k in unclipped:
+                if k == jobs["chains"][0]:
+                    run("vector", vector_between)
                 interleave(k)
                 unquantized.append(k)
-            unclipped.clear()
-            run("vector", vector[2])
+            run("vector", vector_after)
             for t in range(SLOTS):
                 if t == 2:
-                    run("scalar", scalar[1])
+                    run("scalar", scalar_between)
                 relu(m, t)
-                if m in AT_ONCE:
-                    clip(m, t)
-            if m in AT_ONCE:
-                quantize_waiting()
-                interleave(m)
-                unquantized.append(m)
-            else:
-                unclipped.append(m)
-            if m == UNITS - 1:
-                quantize_waiting()
-            run("scalar", scalar[2])
-            run("vector", vector[3])
-            for job in JOBS[m]["tensor"]:
+            run("scalar", scalar_after)
+            for job in jobs["tensor"]:
                 tensor_jobs[job[0]](*job[1:], next_bank())
+        quantize_waiting()
 
         last, a = UNITS - 1, GROUPS - 1
         halves = (slice(0, 256), slice(256, GROUP))

from contextlib import ExitStack

import concourse.mybir as mybir
from concourse.masks import make_identity

F32 = mybir.dt.float32
BF16 = mybir.dt.bfloat16
I32 = mybir.dt.int32
U32 = mybir.dt.uint32
U8 = mybir.dt.uint8
F8 = mybir.dt.float8_e4m3fn
F8X4 = mybir.dt.float8_e4m3fn_x4
F4X4 = mybir.dt.float4_e2m1fn_x4
ALU = mybir.AluOpType
ACT = mybir.ActivationFunctionType

PIXELS, C_IN, HIDDEN, C_OUT = 1536, 1024, 2048, 512
P = 128
SLOTS = 4
K_PASS = P * SLOTS
PASSES = C_IN // K_PASS
BUNDLES = HIDDEN // K_PASS
GROUP = 512
GROUPS = PIXELS // GROUP
TILES = GROUP // P
ROW_TILES = C_OUT // P
BLOCK = 128
UNITS = GROUPS * BUNDLES

FLOPS = 2 * PIXELS * HIDDEN * (C_IN + C_OUT)

JOBS = (
    {
        "tensor": (("x_turn", 1, 0), ("x_turn", 1, 1), ("x_turn", 1, 2), ("w2_turn", 0, 0)),
        "scalar": ((("x_widen", 1, 2), ("x_widen", 1, 0)), (), ()),
        "chains": (),
        "vector": (
            (("x_widen", 1, 1), ("x_widen", 1, 3), ("vectors",), ("w1", 1), ("w2_widen", 0, 0), ("w2_widen", 1, 0)),
            (),
            (),
        ),
    },
    {
        "tensor": (("w2_turn", 1, 0), ("x_turn", 1, 3), ("w2_turn", 0, 1)),
        "scalar": ((("x_out", 1, 1), ("x_out", 1, 0)), (("x_out", 1, 2),), (("w2_out", 0, 0),)),
        "chains": (0,),
        "vector": ((("w2_widen", 0, 1),), (("w2_widen", 3, 1), ("w1", 2)), (("w2_widen", 2, 0),)),
    },
    {
        "tensor": (("w2_turn", 2, 0), ("w2_turn", 3, 1)),
        "scalar": ((), (("w2_out", 1, 0), ("w2_out", 0, 1)), ()),
        "chains": (),
        "vector": ((("x_out", 1, 3), ("w1", 3)), (), ()),
    },
    {
        "tensor": (),
        "scalar": ((), (), (("w2_out", 3, 1),)),
        "chains": (1, 2),
        "vector": (
            (("w2_widen", 3, 0), ("x_quant", 1, 1), ("x_quant", 1, 0), ("w2_widen", 2, 1), ("w2_widen", 1, 1)),
            (),
            (("x_widen", 2, 1),),
        ),
    },
    {
        "tensor": (("w2_turn", 2, 1), ("w2_turn", 1, 1), ("w2_turn", 3, 0)),
        "scalar": ((("w2_out", 2, 0),), (("x_widen", 2, 2),), ()),
        "chains": (),
        "vector": ((("x_widen", 2, 0),), (), ()),
    },
    {
        "tensor": (("x_turn", 2, 0), ("x_turn", 2, 1), ("x_turn", 2, 2)),
        "scalar": ((("w2_out", 2, 1), ("w2_out", 1, 1)), (), ()),
        "chains": (),
        "vector": ((("x_widen", 2, 3), ("w2_quant", 0), ("w2_out", 3, 0)), (), ()),
    },
    {
        "tensor": (("x_turn", 2, 3),),
        "scalar": ((), (("x_out", 2, 2),), (("x_out", 2, 0),)),
        "chains": (3,),
        "vector": ((), (("w2_quant", 3),), ()),
    },
    {
        "tensor": (("y_sum", 0, 0), ("y_sum", 0, 1), ("y_sum", 0, 2)),
        "scalar": ((("x_out", 2, 3), ("x_out", 2, 1)), (), ()),
        "chains": (4,),
        "vector": ((("w2_quant", 2),), (("w2_quant", 1),), (("x_quant", 2, 1), ("x_quant", 2, 0))),
    },
    {
        "tensor": (),
        "scalar": ((), (), ()),
        "chains": (5,),
        "vector": ((), (), ()),
    },
    {
        "tensor": (("y_sum", 0, 3),),
        "scalar": ((("y_out", 0, 2),), (), (("y_out", 0, 0),)),
        "chains": (6, 7),
        "vector": ((), (), ()),
    },
    {
        "tensor": (("y_sum", 1, 0), ("y_sum", 1, 1), ("y_sum", 1, 2), ("y_sum", 1, 3)),
        "scalar": ((), (("y_out", 0, 3), ("y_out", 0, 1)), ()),
        "chains": (8,),
        "vector": ((), (), ()),
    },
    {
        "tensor": (),
        "scalar": ((("y_out", 1, 0), ("y_out", 1, 1), ("y_out", 1, 2), ("y_out", 1, 3)), (), ()),
        "chains": (9, 10),
        "vector": ((), (), ()),
    },
)


def tile_clipped_pointwise_pair_d6_kernel(
    tc, x_bytes, x_scale, w1_words, w1_scales, scale, shift, cap, w2_bytes, w2_scale, out
):
    nc = tc.nc
    with ExitStack() as ctx:
        keep = ctx.enter_context(tc.tile_pool(name="keep", bufs=1))
        work = ctx.enter_context(tc.tile_pool(name="work", bufs=3))
        psum = ctx.enter_context(tc.psum_pool(name="psum", bufs=1))
        ctx.enter_context(tc.manual_schedule())

        turn_order = ("x0", "x1", "y0", "y1")
        turns = []

        def next_bank():
            turns.append(turn_order[len(turns) % 4])
            return turns[-1]

        def kept(shape, dtype, name):
            return keep.tile(shape, dtype, name=name, align_bytes=64)

        xb = [kept([P, TILES, C_IN], U8, "xb%d" % a) for a in range(GROUPS)]
        xs = kept([P, GROUPS, TILES * C_IN // BLOCK], F32, "xs")
        w1_raw = [kept([P, PASSES, 2 * K_PASS], U8, "w1_raw%d" % f) for f in range(BUNDLES)]
        w1s_raw = kept([P, PASSES, HIDDEN], U8, "w1s_raw")
        w2b = [kept([P, 2, HIDDEN], U8, "w2b%d" % h) for h in range(2)]
        w2s = kept([P, ROW_TILES * HIDDEN // BLOCK], F32, "w2s")
        vec_rows = kept([P, K_PASS], BF16, "vec_rows")
        ident = kept([P, P], F32, "ident")

        nc.vector.memset(vec_rows[:], 0.0)
        nc.vector.memset(w1s_raw[:].rearrange("p g n -> p (g n)").bitcast(I32), 0)
        make_identity(nc, ident[:])

        x_src = x_bytes.rearrange("(a h p n) k -> a h p n k", h=2, p=P, n=2)
        w1_src = w1_words.bitcast(I32)
        w1s_src = w1_scales.bitcast(I32)
        w1s_words = w1s_raw[:].bitcast(I32)
        w2_src = w2_bytes.rearrange("(h i p) k -> h p i k", h=2, p=P)

        def load_x(a):
            nc.sync.dma_start(
                out=xb[a][:].rearrange("p (h n) k -> p h (n k)", h=2), in_=x_src[a].rearrange("h p n k -> p h (n k)")
            )

        def load_w1(f):
            nc.sync.dma_start(
                out=w1_raw[f][:].bitcast(I32), in_=w1_src[:, :, 256 * f : 256 * f + 256].rearrange("g p c -> p g c")
            )

        nc.sync.dma_start(out=xb[0][:, 0:2, :], in_=x_src[0, 0])
        nc.scalar.dma_start(
            out=xs[:].rearrange("p a (h c) -> p (a h) c", h=2),
            in_=x_scale.rearrange("(a h p n) j -> p (a h) (n j)", h=2, p=P, n=2),
        )
        nc.sync.dma_start(out=xb[0][:, 2:4, :], in_=x_src[0, 1])
        load_w1(0)
        for q in range(4):
            nc.sync.dma_start(
                out=w1s_words[32 * q : 32 * q + 4, :, :],
                in_=w1s_src[:, 4 * q : 4 * q + 4, :].rearrange("g r c -> r g c"),
            )
        load_x(1)
        for v, vec in enumerate((scale, shift, cap)):
            nc.sync.dma_start(
                out=vec_rows[BUNDLES * v : BUNDLES * v + BUNDLES, :], in_=vec.rearrange("(f c) -> f c", f=BUNDLES)
            )
        nc.sync.dma_start(out=w2s[:], in_=w2_scale.rearrange("i j -> (i j)").partition_broadcast(P))
        load_w1(1)
        nc.sync.dma_start(out=w2b[0][:], in_=w2_src[0])
        nc.sync.dma_start(out=w2b[1][:], in_=w2_src[1])
        load_w1(2)
        load_w1(3)
        load_x(2)

        w1c = [kept([P, PASSES, 2 * K_PASS], U8, "w1c%d" % f) for f in range(BUNDLES)]
        w1s = [kept([P, PASSES, K_PASS], U8, "w1s%d" % f) for f in range(BUNDLES)]
        w2q = [kept([P, C_OUT], U32, "w2q%d" % f) for f in range(BUNDLES)]
        w2qs = [kept([P, C_OUT], U8, "w2qs%d" % f) for f in range(BUNDLES)]
        xq = [kept([P, PASSES, GROUP], U32, "xq%d" % a) for a in range(GROUPS)]
        xqs = [kept([P, PASSES, GROUP], U8, "xqs%d" % a) for a in range(GROUPS)]

        def w1_words_permute(f):
            nc.vector.tensor_copy(
                out=w1c[f][:].bitcast(I32).rearrange("p g (t c j) -> p g t c j", t=SLOTS, c=32),
                in_=w1_raw[f][:].bitcast(I32).rearrange("p g (c t j) -> p g t c j", t=SLOTS, c=32),
            )

        def w1_scales_permute(f):
            nc.vector.tensor_copy(
                out=w1s[f][:].bitcast(I32).rearrange("p g (t c) -> p g t c", t=SLOTS),
                in_=w1s_words[:, :, 128 * f : 128 * f + 128].rearrange("p g (c t) -> p g t c", t=SLOTS),
            )

        def w1_permute(engine, f):
            w1_scales_permute(f)
            w1_words_permute(f)

        vec_turned = kept([P, SLOTS, P], F32, "vec_turned")
        vecs = kept([P, SLOTS, 3 * BUNDLES], F32, "vecs")
        vec_bank = []

        def vectors_permute():
            nc.vector.tensor_copy(
                out=vec_turned[:].rearrange("p t (c i) -> p t c i", c=32),
                in_=vec_rows[:].rearrange("p (c t i) -> p t c i", t=SLOTS, c=32),
            )

        def vectors_turn():
            bank = psum.tile([P, SLOTS, P], F32, name="vec_bank", tag="x0")
            vec_bank.append(bank)
            for t in range(SLOTS):
                nc.tensor.transpose(bank[:, t, :], vec_turned[:, t, :], ident[:])

        def vectors_out(engine):
            nc.vector.tensor_copy(out=vecs[:], in_=vec_bank[0][:, :, 0 : 3 * BUNDLES])

        def scale_of(f, t):
            return vecs[:, t, f : f + 1]

        def shift_of(f, t):
            return vecs[:, t, BUNDLES + f : BUNDLES + f + 1]

        def cap_of(f, t):
            return vecs[:, t, 2 * BUNDLES + f : 2 * BUNDLES + f + 1]

        x_wide = {}
        x_split = set()
        x_bank = {}
        x_grouped = {}

        def copy(engine, out_, in_):
            if engine == "vector":
                nc.vector.tensor_copy(out=out_, in_=in_)
            else:
                nc.scalar.copy(out=out_, in_=in_)

        def x_widen(engine, a, n, blocks=range(C_IN // BLOCK)):
            if (a, n) not in x_wide:
                x_wide[a, n] = work.tile([P, C_IN], BF16, name="x_wide", bufs=5, align_bytes=64)
            wide = x_wide[a, n]
            for j in blocks:
                src = xb[a][:, n, BLOCK * j : BLOCK * j + BLOCK].bitcast(F8)
                factor = xs[:, a, 8 * n + j : 8 * n + j + 1]
                if engine == "vector":
                    g, q = j // 4, j % 4
                    x_split.add((a, n, g))
                    halves = wide[:, K_PASS * g : K_PASS * (g + 1)].rearrange("p (u c e) -> p c u e", u=2, e=2)
                    nc.vector.tensor_scalar(
                        out=halves[:, 32 * q : 32 * q + 32, :, :],
                        in0=src.rearrange("p (c u e) -> p c u e", u=2, e=2),
                        scalar1=factor,
                        scalar2=None,
                        op0=ALU.mult,
                    )
                else:
                    nc.scalar.activation(
                        out=wide[:, BLOCK * j : BLOCK * j + BLOCK], in_=src, func=ACT.Copy, scale=factor
                    )

        def x_turn(a, n, tag):
            words = x_wide[a, n][:].bitcast(F32)
            bank = psum.tile([P, 4, P], F32, name="x_bank_" + tag, tag=tag)
            x_bank[a, n] = bank
            for g in range(PASSES):
                for u in range(2):
                    if (a, n, g) in x_split:
                        src = words[:, 256 * g + 128 * u : 256 * g + 128 * u + 128]
                    else:
                        src = words[:, 256 * g + u : 256 * (g + 1) : 2]
                    nc.tensor.transpose(bank[:, 2 * g + u, :], src, ident[:])

        def x_out(engine, a, n):
            if a not in x_grouped:
                x_grouped[a] = work.tile([P, PASSES, SLOTS * GROUP], BF16, name="x_grouped", bufs=2, align_bytes=64)
            words = x_grouped[a][:].bitcast(F32)[:, :, 256 * n : 256 * n + 256]
            copy(
                engine,
                words.rearrange("p g (r u) -> p g r u", u=2),
                x_bank[a, n][:].rearrange("p (g u) r -> p g r u", g=PASSES),
            )

        def x_quant(engine, a, g):
            nc.vector.quantize_mx(out=xq[a][:, g, :].bitcast(F8X4), scales=xqs[a][:, g, :], in_=x_grouped[a][:, g, :])

        def x_quant_tile(a, n):
            c = slice(P * n, P * n + P)
            for g in range(PASSES):
                nc.vector.quantize_mx(
                    out=xq[a][:, g, c].bitcast(F8X4),
                    scales=xqs[a][:, g, c],
                    in_=x_grouped[a][:, g, SLOTS * P * n : SLOTS * P * (n + 1)],
                )

        w2_wide = {}
        w2_bank = {}
        w2_grouped = {}

        def w2_widen(engine, f, h):
            for r in range(2):
                wide = work.tile([P, K_PASS], BF16, name="w2_wide", bufs=8, align_bytes=64)
                w2_wide[f, h, r] = wide
                for q in range(4):
                    k0 = K_PASS * f + BLOCK * q
                    j = (2 * h + r) * (HIDDEN // BLOCK) + 4 * f + q
                    nc.vector.tensor_scalar(
                        out=wide[:, BLOCK * q : BLOCK * q + BLOCK].rearrange("p (c i t) -> p c t i", c=8, i=4),
                        in0=w2b[h][:, r, k0 : k0 + BLOCK].bitcast(F8).rearrange("p (c t i) -> p c t i", c=8, i=4),
                        scalar1=w2s[:, j : j + 1],
                        scalar2=None,
                        op0=ALU.mult,
                    )

        def w2_turn(f, h, tag):
            bank = psum.tile([P, 4, P], F32, name="w2_bank_" + tag, tag=tag)
            w2_bank[f, h] = bank
            for r in range(2):
                words = w2_wide[f, h, r][:].bitcast(F32)
                for u in range(2):
                    nc.tensor.transpose(bank[:, 2 * r + u, :], words[:, u::2], ident[:])

        def w2_out(engine, f, h):
            if f not in w2_grouped:
                w2_grouped[f] = work.tile([P, SLOTS * C_OUT], BF16, name="w2_grouped", bufs=4, align_bytes=64)
            words = w2_grouped[f][:].bitcast(F32)[:, 512 * h : 512 * h + 512]
            copy(
                engine,
                words.rearrange("p (r c u) -> p r c u", r=2, u=2),
                w2_bank[f, h][:].rearrange("p (r u) c -> p r c u", r=2),
            )

        def w2_quant(engine, f):
            nc.vector.quantize_mx(out=w2q[f][:].bitcast(F8X4), scales=w2qs[f][:], in_=w2_grouped[f][:])

        z = {}
        planes = {}
        grouped = {}
        hq = {}
        hqs = {}

        def z_sum(a, f, columns):
            for t in range(SLOTS):
                for g in range(PASSES):
                    nc.tensor.matmul_mx(
                        out=z[t][:, columns],
                        lhsT=w1c[f][:, g, 2 * P * t : 2 * P * (t + 1)].bitcast(F4X4),
                        lhsT_scale=w1s[f][:, g, P * t : P * (t + 1)],
                        rhs=xq[a][:, g, columns].bitcast(F8X4),
                        rhs_scale=xqs[a][:, g, columns],
                        start=(g == 0),
                        stop=(g == PASSES - 1),
                    )

        def z_banks():
            for t in range(SLOTS):
                z[t] = psum.tile([P, GROUP], F32, name="z%d" % t, tag="z%d" % t)

        def relu(m, t):
            f = m % BUNDLES
            if m not in planes:
                planes[m] = work.tile([P, SLOTS, GROUP], BF16, name="planes", bufs=5, align_bytes=64)
            nc.scalar.activation(
                out=planes[m][:, t, :], in_=z[t][:], func=ACT.Relu, bias=shift_of(f, t), scale=scale_of(f, t)
            )

        def clip(m, t, c0=0, c1=GROUP):
            part = planes[m][:, t, c0:c1]
            nc.vector.tensor_scalar(
                out=part, in0=part, scalar1=0.0, scalar2=cap_of(m % BUNDLES, t), op0=ALU.max, op1=ALU.min
            )

        def interleave(m, c0=0, c1=GROUP):
            if m not in grouped:
                grouped[m] = work.tile([P, SLOTS * GROUP], BF16, name="grouped", align_bytes=64)
            nc.vector.tensor_copy(
                out=grouped[m][:, SLOTS * c0 : SLOTS * c1].rearrange("p (c i t) -> p c t i", i=4, t=SLOTS),
                in_=planes[m][:, :, c0:c1].rearrange("p t (c i) -> p c t i", i=4),
            )

        def h_quant(m, c0=0, c1=GROUP):
            if m not in hq:
                hq[m] = work.tile([P, GROUP], U32, name="hq", bufs=9, align_bytes=64)
                hqs[m] = work.tile([P, GROUP], U8, name="hqs", bufs=9, align_bytes=64)
            nc.vector.quantize_mx(
                out=hq[m][:, c0:c1].bitcast(F8X4), scales=hqs[m][:, c0:c1], in_=grouped[m][:, SLOTS * c0 : SLOTS * c1]
            )

        y = {}

        def y_pass(bank, a, i, f, c0=0, c1=GROUP):
            m = BUNDLES * a + f
            nc.tensor.matmul_mx(
                out=bank[:],
                lhsT=w2q[f][:, P * i : P * (i + 1)].bitcast(F8X4),
                lhsT_scale=w2qs[f][:, P * i : P * (i + 1)],
                rhs=hq[m][:, c0:c1].bitcast(F8X4),
                rhs_scale=hqs[m][:, c0:c1],
                start=(f == 0),
                stop=(f == BUNDLES - 1),
            )

        def y_sum(a, i, tag):
            y[a, i] = psum.tile([P, GROUP], F32, name="y_" + tag, tag=tag)
            for f in range(BUNDLES):
                y_pass(y[a, i], a, i, f)

        def y_out(engine, a, i):
            rows = work.tile([P, GROUP], F32, name="y_rows", bufs=4, align_bytes=64)
            copy(
                engine,
                rows[:].rearrange("m (h r n) -> m h r n", h=2, n=2),
                y[a, i][:].rearrange("m (h n r) -> m h r n", h=2, n=2),
            )
            nc.sync.dma_start(out=out[P * i : P * (i + 1), GROUP * a : GROUP * (a + 1)], in_=rows[:])

        def y_half_out(engine, bank, a, i, h):
            rows = work.tile([P, 256], F32, name="y_half", bufs=8, align_bytes=64)
            copy(engine, rows[:].rearrange("m (r n) -> m r n", n=2), bank[:].rearrange("m (n r) -> m r n", n=2))
            c0 = GROUP * a + 256 * h
            nc.sync.dma_start(out=out[P * i : P * (i + 1), c0 : c0 + 256], in_=rows[:])

        x_widen("vector", 0, 0)
        x_widen("scalar", 0, 1)
        x_turn(0, 0, "x0")
        x_widen("vector", 0, 2)
        x_out("vector", 0, 0)
        x_turn(0, 1, "x1")
        x_widen("vector", 0, 3, range(0, 4))
        x_widen("scalar", 0, 3, range(4, 8))
        x_turn(0, 2, "y0")
        x_quant_tile(0, 0)
        x_out("scalar", 0, 1)
        w1_words_permute(0)
        w1_scales_permute(0)
        x_out("vector", 0, 2)
        x_turn(0, 3, "y1")
        z_banks()
        z_sum(0, 0, slice(0, P))
        x_quant_tile(0, 1)
        z_sum(0, 0, slice(P, 2 * P))
        x_out("scalar", 0, 3)
        x_quant_tile(0, 2)
        x_quant_tile(0, 3)
        vectors_permute()
        vectors_turn()
        z_sum(0, 0, slice(2 * P, 3 * P))
        z_sum(0, 0, slice(3 * P, 4 * P))

        engine_jobs = {
            "x_widen": x_widen,
            "x_out": x_out,
            "x_quant": x_quant,
            "w1": w1_permute,
            "w2_widen": w2_widen,
            "w2_out": w2_out,
            "w2_quant": w2_quant,
            "vectors": vectors_out,
            "y_out": y_out,
        }
        tensor_jobs = {"x_turn": x_turn, "w2_turn": w2_turn, "y_sum": y_sum}

        def run(engine, jobs):
            for job in jobs:
                engine_jobs[job[0]](engine, *job[1:])

        unquantized = []

        def quantize_waiting():
            for k in unquantized:
                h_quant(k)
            unquantized.clear()

        for m in range(UNITS):
            jobs = JOBS[m]
            scalar_before, scalar_between, scalar_after = jobs["scalar"]
            vector_before, vector_between, vector_after = jobs["vector"]
            run("scalar", scalar_before)
            if m > 0:
                z_banks()
                z_sum(m // BUNDLES, m % BUNDLES, slice(0, GROUP))
            run("vector", vector_before)
            for k in jobs["chains"]:
                for t in range(SLOTS):
                    clip(k, t)
                quantize_waiting()
                if k == jobs["chains"][0]:
                    run("vector", vector_between)
                interleave(k)
                unquantized.append(k)
            run("vector", vector_after)
            for t in range(SLOTS):
                if t == 2:
                    run("scalar", scalar_between)
                relu(m, t)
            run("scalar", scalar_after)
            for job in jobs["tensor"]:
                tensor_jobs[job[0]](*job[1:], next_bank())
        quantize_waiting()

        last, a = UNITS - 1, GROUPS - 1
        halves = (slice(0, 256), slice(256, GROUP))
        for t in range(SLOTS):
            clip(last, t, 0, 256)
        interleave(last, 0, 256)
        for t in range(SLOTS):
            clip(last, t, 256, GROUP)
        h_quant(last, 0, 256)
        interleave(last, 256, GROUP)
        y_half = {}
        for h in range(2):
            for i in range(ROW_TILES):
                tag = next_bank() if h == 0 else "z%d" % i
                y_half[h, i] = psum.tile([P, 256], F32, name="y_half_" + tag, tag=tag)
                for f in range(BUNDLES - 1):
                    y_pass(y_half[h, i], a, i, f, halves[h].start, halves[h].stop)
        for h in range(2):
            if h == 1:
                h_quant(last, 256, GROUP)
            for i in range(ROW_TILES):
                y_pass(y_half[h, i], a, i, BUNDLES - 1, halves[h].start, halves[h].stop)
                y_half_out("vector" if h == 1 and i % 2 == 1 else "scalar", y_half[h, i], a, i, h)
